import numpy as np
import ml_dtypes


def mxq(x, axis, fmt="e4m3"):
    dtype, down = {"e4m3": (ml_dtypes.float8_e4m3fn, 7), "e5m2": (ml_dtypes.float8_e5m2, 14)}[fmt]
    v = np.moveaxis(np.asarray(x, np.float32).astype(ml_dtypes.bfloat16).astype(np.float64), axis, -1)
    blocks = v.reshape(v.shape[:-1] + (-1, 32))
    amax = np.abs(blocks).max(-1, keepdims=True)
    byte = np.maximum(np.where(amax > 0, np.frexp(amax)[1] - 1 + 127, 0) - down, 1)
    scale = np.exp2(byte - 127.0)
    codes = (blocks / scale).astype(np.float32).astype(dtype).astype(np.float64)
    return np.moveaxis((codes * scale).reshape(v.shape), -1, axis)


WIDE = False


def mx_kscale(k):
    if not WIDE:
        return np.ones(k)
    levels = np.array([30, -30])
    if k % 512:
        return np.exp2(np.random.permutation(np.resize(levels, k // 32))).repeat(32)
    a = np.empty((k // 512, 16))
    for p in range(k // 512):
        a[p, :8] = np.random.permutation(np.resize(levels, 8))
        for g in range(8):
            far = levels[np.abs(levels - a[p, g]) >= 10]
            a[p, g + 8] = far[np.random.randint(len(far))]
    return np.exp2(a.ravel()).repeat(32)


def f64(x):
    return np.asarray(x).astype(np.float64)


def striped(idx):
    return np.tile(idx.reshape(-1, 16).T, (8, 1)).astype(np.uint16)


def unstriped(offs):
    return offs[:16].T.reshape(-1).astype(np.int64)


E2M1 = np.array([0.0, 0.5, 1.0, 1.5, 2.0, 3.0, 4.0, 6.0, -0.0, -0.5, -1.0, -1.5, -2.0, -3.0, -4.0, -6.0])


def pack_weight(w, fmt):
    k, n = w.shape
    w = f64(np.asarray(w, np.float32).astype(ml_dtypes.bfloat16)).reshape(k // 32, 32, n)
    amax = np.abs(w).max(1)
    if fmt == "e4m3":
        byte = np.frexp(amax)[1] - 1 + 127 - 7
    else:
        mant, ex = np.frexp(amax / 6.0)
        byte = np.where(mant > 0.5, ex, ex - 1) + 127
    byte = np.clip(np.where(amax > 0, byte, 1), 1, 254)
    scaled = (w * np.exp2(127.0 - byte)[:, None, :]).reshape(k, n).astype(np.float32)
    by_word = np.ascontiguousarray(scaled.reshape(k // 512, 128, 4, n).transpose(0, 1, 3, 2))
    if fmt == "e4m3":
        words = by_word.astype(ml_dtypes.float8_e4m3fn).view(np.uint8)
    else:
        c = by_word.astype(ml_dtypes.float4_e2m1fn).view(np.uint8) & 0xF
        words = (c[..., 0::2] | (c[..., 1::2] << 4)).reshape(k // 512, 128, 2 * n)
    return np.ascontiguousarray(words), np.ascontiguousarray(byte.astype(np.uint8).reshape(k // 512, 16, n))


def unpack_weight(words, scales, fmt):
    g, _, n = scales.shape
    words = np.ascontiguousarray(words).reshape(g, 128, n, -1)
    if fmt == "e4m3":
        vals = words.view(ml_dtypes.float8_e4m3fn).astype(np.float64)
    else:
        nib = np.empty((g, 128, n, 4), np.uint8)
        nib[..., 0::2] = words & 0xF
        nib[..., 1::2] = words >> 4
        vals = E2M1[nib]
    vals = vals * np.repeat(np.exp2(scales.astype(np.float64) - 127.0), 8, axis=1)[..., None]
    return vals.transpose(0, 1, 3, 2).reshape(g * 512, n)


def d_relu2(v):
    return 2.0 * np.maximum(v, 0.0)


K, T, E, C, H, N = 128, 1024, 4, 512, 512, 1536


def by_expert(wq, xq):
    return np.concatenate([wq[e].T @ xq[:, e * C:(e + 1) * C] for e in range(E)], axis=1)


def setup_inputs():
    n = np.random.standard_normal
    s = mx_kscale(N)[:, None]
    u = mx_kscale(H)
    first = np.random.permutation(np.repeat(np.arange(E), T // E))
    second = (first + 1 + np.random.permutation(np.repeat(np.arange(E - 1), -(-T // (E - 1)))[:T])) % E
    while np.bincount(second, minlength=E).max() != T // E:
        load = np.bincount(second, minlength=E); hi, lo = int(load.argmax()), int(load.argmin())
        t = np.flatnonzero((second == hi) & (first != lo))[0]; second[t] = lo
    slot_token = np.empty(E * C, np.int64); pos = np.empty((2, T), np.int64); fill = np.zeros(E, np.int64)
    place = np.stack([np.random.permutation(C) for _ in range(E)])
    for r, deal in enumerate((first, second)):
        for t in np.random.permutation(T):
            e = deal[t]; j = e * C + place[e, fill[e]]; fill[e] += 1; slot_token[j] = t; pos[r, t] = j
    g = np.random.uniform(0.2, 0.8, T)
    w_slot = np.empty(E * C); w_slot[pos[0]] = g; w_slot[pos[1]] = 1.0 - g
    w2 = [pack_weight(m, "e2m1") for m in n((E, N, H)) / np.sqrt(N) / s[None] * u[None, None, :]]
    w1 = [pack_weight(m, "e2m1") for m in n((E, H, K)) / np.sqrt(H) / u[None, :, None]]
    return {
        "dyT": (n((N, T)) * s).astype(np.float32),
        "a": n((H, E * C)).astype(np.float32),
        "w2_words": np.stack([m[0] for m in w2]),
        "w2_scales": np.stack([m[1] for m in w2]),
        "w1_words": np.stack([m[0] for m in w1]),
        "w1_scales": np.stack([m[1] for m in w1]),
        "gate": np.tile(w_slot, (N, 1)).astype(np.float32),
        "offs": striped(slot_token),
        "pos1": striped(pos[0]),
        "pos2": striped(pos[1]),
    }


def reference(dyT, a, w2_words, w2_scales, w1_words, w1_scales, gate, offs, pos1, pos2):
    idx = unstriped(offs)
    w2 = np.stack([unpack_weight(w2_words[e], w2_scales[e], "e2m1") for e in range(E)])
    w1 = np.stack([unpack_weight(w1_words[e], w1_scales[e], "e2m1") for e in range(E)])
    gq = mxq(f64(gate) * f64(dyT)[:, idx], 0, "e5m2")
    dh = by_expert(w2, gq)
    da = dh * d_relu2(f64(a))
    dx = by_expert(w1, mxq(da, 0, "e5m2"))
    return dx[:, unstriped(pos1)] + dx[:, unstriped(pos2)]

@@ -1,0 +1,288 @@
+from contextlib import ExitStack
+
+import concourse.mybir as mybir
+from concourse.masks import make_identity
+
+K, T, E, C, H, N = 128, 1024, 4, 512, 512, 1536
+P = 128
+PACK = 4
+SLOTS = E * C
+PASSES = N // 512
+QT = C // P
+
+FLOPS = 2 * SLOTS * (N * H + H * K)
+BYTES = (
+    4 * N * T + 4 * H * SLOTS + E * PASSES * (128 * 1024 + 16 * 512)
+    + E * (128 * 256 + 16 * 128) + 4 * SLOTS + 2 * 128 * (128 + 64 + 64) + 4 * K * T
+)
+
+F32 = mybir.dt.float32
+BF16 = mybir.dt.bfloat16
+I32 = mybir.dt.int32
+U32 = mybir.dt.uint32
+U16 = mybir.dt.uint16
+U8 = mybir.dt.uint8
+E5M2 = mybir.dt.float8_e5m2_x4
+E2M1 = mybir.dt.float4_e2m1fn_x4
+MULT = mybir.AluOpType.mult
+ADD = mybir.AluOpType.add
+COPY = mybir.ActivationFunctionType.Copy
+RELU = mybir.ActivationFunctionType.Relu
+
+
+def tile_moe_bdx_mlp_relu2_kernel(
+    tc, dyT, a, w2_words, w2_scales, w1_words, w1_scales, gate, offs, pos1, pos2, out
+):
+    nc = tc.nc
+    with ExitStack() as ctx:
+        keep = ctx.enter_context(tc.tile_pool(name="keep", bufs=1))
+        gathered = ctx.enter_context(tc.tile_pool(name="gathered", bufs=3))
+        grouped = ctx.enter_context(tc.tile_pool(name="grouped", bufs=3))
+        coded = ctx.enter_context(tc.tile_pool(name="coded", bufs=8))
+        hidden = ctx.enter_context(tc.tile_pool(name="hidden", bufs=8))
+        da_pool = ctx.enter_context(tc.tile_pool(name="da_pool", bufs=2))
+        dh_psum = ctx.enter_context(tc.psum_pool(name="dh_psum", bufs=1))
+        tr_psum = ctx.enter_context(tc.psum_pool(name="tr_psum", bufs=2))
+        dx_psum = ctx.enter_context(tc.psum_pool(name="dx_psum", bufs=2))
+
+        offs_sb = keep.tile([P, SLOTS // 16], U16, name="offs_sb")
+        pos1_sb = keep.tile([P, T // 16], U16, name="pos1_sb")
+        pos2_sb = keep.tile([P, T // 16], U16, name="pos2_sb")
+        gates = [keep.tile([P, C], F32, name=f"gate{e}") for e in range(E)]
+        planes = [
+            [keep.tile([P, T], F32, name=f"dy{s}_{t}") for t in range(PACK)] for s in range(PASSES)
+        ]
+        w2_sb = [keep.tile([P, PASSES * 1024], U8, name=f"w2_{e}", align_bytes=64) for e in range(E)]
+        w2_sc = keep.tile([P, E * PASSES * H], U8, name="w2_sc", align_bytes=64)
+        w1_sb = keep.tile([P, E * 256], U8, name="w1_sb", align_bytes=64)
+        w1_sc = keep.tile([P, E * K], U8, name="w1_sc", align_bytes=64)
+        a_sb = [keep.tile([P, PACK, C], F32, name=f"a{e}") for e in range(E)]
+        ident = keep.tile([P, P], F32, name="ident")
+        dx_sb = keep.tile([P, SLOTS], F32, name="dx_sb")
+        first = keep.tile([P, T], F32, name="first")
+        second = keep.tile([P, T], F32, name="second")
+        total = keep.tile([P, T], F32, name="total")
+
+        nc.gpsimd.memset(w2_sc[:].bitcast(I32), 0)
+        nc.gpsimd.memset(w1_sc[:].bitcast(I32), 0)
+        make_identity(nc, ident[:])
+
+        dy_rows = dyT.rearrange("(s p t) j -> s t p j", p=P, t=PACK)
+
+        def load_pass(s):
+            for t in range(PACK):
+                nc.sync.dma_start(out=planes[s][t][:], in_=dy_rows[s, t])
+
+        def load_gate(e):
+            nc.sync.dma_start(out=gates[e][:], in_=gate[0:P, e * C : (e + 1) * C])
+
+        def load_w2(e):
+            nc.sync.dma_start(
+                out=w2_sb[e][:].bitcast(I32).rearrange("p (s w) -> p s w", s=PASSES),
+                in_=w2_words.bitcast(I32)[e].rearrange("s p w -> p s w"),
+            )
+
+        def load_a(e):
+            nc.sync.dma_start(
+                out=a_sb[e][:], in_=a[:, e * C : (e + 1) * C].rearrange("(p t) c -> p t c", t=PACK)
+            )
+
+        def load_scales():
+            src2 = w2_scales.bitcast(I32).rearrange("e s f w -> f (e s) w")
+            src1 = w1_scales.bitcast(I32).rearrange("e s f w -> f (e s) w")
+            for q in range(4):
+                rows = slice(32 * q, 32 * q + 4)
+                nc.sync.dma_start(
+                    out=w2_sc[rows, :].bitcast(I32).rearrange("f (g w) -> f g w", g=E * PASSES),
+                    in_=src2[4 * q : 4 * q + 4],
+                )
+            for q in range(4):
+                rows = slice(32 * q, 32 * q + 4)
+                nc.sync.dma_start(
+                    out=w1_sc[rows, :].bitcast(I32).rearrange("f (g w) -> f g w", g=E),
+                    in_=src1[4 * q : 4 * q + 4],
+                )
+
+        nc.sync.dma_start(offs_sb[:], offs)
+        load_gate(0)
+        load_pass(0)
+        load_gate(1)
+        load_scales()
+        load_w2(0)
+        load_pass(1)
+        load_w2(1)
+        load_pass(2)
+        nc.sync.dma_start(
+            out=w1_sb[:].bitcast(I32).rearrange("p (e w) -> p e w", e=E),
+            in_=w1_words.bitcast(I32).rearrange("e s p w -> p (e s) w"),
+        )
+        load_a(0)
+        load_gate(2)
+        load_gate(3)
+        load_a(1)
+        load_w2(2)
+        load_w2(3)
+        load_a(2)
+        load_a(3)
+        nc.sync.dma_start(pos1_sb[:], pos1)
+        nc.sync.dma_start(pos2_sb[:], pos2)
+
+        g32 = {}
+        codes = {}
+        dh_banks = {}
+        dh_out = {}
+        slopes = {}
+        da_codes = {}
+        da_parts = {}
+
+        def gather(e, s, t):
+            if t == 0:
+                g32[e, s] = gathered.tile([P, PACK, C], F32, name="g32")
+            nc.vector.tensor_tensor(
+                g32[e, s][:, t, :],
+                planes[s][t][:].indirect(offs_sb[:, e * (C // 16) : (e + 1) * (C // 16)]),
+                gates[e][:],
+                MULT,
+            )
+
+        def interleave(e, s):
+            gb = grouped.tile([P, C, PACK], BF16, name="gb", align_bytes=64)
+            g32[e, s, "b"] = gb
+            nc.scalar.activation(
+                gb[:].rearrange("p (c i) t -> p c t i", i=4),
+                g32[e, s][:].rearrange("p t (c i) -> p c t i", i=4),
+                COPY,
+            )
+
+        def quantise(e, s):
+            words = coded.tile([P, C], U32, name="g_words", align_bytes=64)
+            scales = coded.tile([P, C], U8, name="g_scales", align_bytes=64)
+            codes[e, s] = (words, scales)
+            nc.vector.quantize_mx(
+                out=words[:].bitcast(E5M2),
+                scales=scales[:],
+                in_=g32[e, s, "b"][:].rearrange("p c t -> p (c t)"),
+            )
+
+        def multiply2(e, s):
+            words, scales = codes[e, s]
+            for q in range(QT):
+                if s == 0:
+                    dh_banks[e, q] = dh_psum.tile([P, H], F32, name=f"dh{q}")
+                cols = slice(q * P, (q + 1) * P)
+                nc.tensor.matmul_mx(
+                    out=dh_banks[e, q][:],
+                    lhsT=words[:, cols].bitcast(E5M2),
+                    lhsT_scale=scales[:, cols],
+                    rhs=w2_sb[e][:, s * 1024 : (s + 1) * 1024].bitcast(E2M1),
+                    rhs_scale=w2_sc[:, (e * PASSES + s) * H : (e * PASSES + s + 1) * H],
+                    start=(s == 0),
+                    stop=(s == PASSES - 1),
+                )
+
+        def slope(e):
+            slopes[e] = da_pool.tile([P, C, PACK], F32, name="slope")
+            nc.scalar.activation(
+                slopes[e][:], a_sb[e][:].rearrange("p t c -> p c t"), RELU, scale=2.0
+            )
+
+        def empty_dh(e):
+            for q in range(QT):
+                dh_out[e, q] = hidden.tile([P, PACK, P], F32, name="dh_out")
+                nc.scalar.activation(
+                    dh_out[e, q][:], dh_banks[e, q][:].rearrange("p (m t) -> p t m", t=PACK), COPY
+                )
+
+        def da_part(e, q):
+            if q == 0:
+                da_parts[e] = da_pool.tile([P, C, PACK], BF16, name="da", align_bytes=64)
+            turned = tr_psum.tile([P, PACK, P], F32, name="turned")
+            for t in range(PACK):
+                nc.tensor.transpose(turned[:, t, :], dh_out[e, q][:, t, :], ident[:])
+            cols = slice(q * P, (q + 1) * P)
+            nc.vector.tensor_tensor(
+                da_parts[e][:, cols, :],
+                slopes[e][:, cols, :],
+                turned[:].rearrange("p t c -> p c t"),
+                MULT,
+            )
+
+        def finish(e):
+            words = da_pool.tile([P, C], U32, name="da_words", align_bytes=64)
+            scales = da_pool.tile([P, C], U8, name="da_scales", align_bytes=64)
+            nc.vector.quantize_mx(
+                out=words[:].bitcast(E5M2),
+                scales=scales[:],
+                in_=da_parts[e][:].rearrange("p c t -> p (c t)"),
+            )
+            dx = dx_psum.tile([P, C], F32, name="dx")
+            nc.tensor.matmul_mx(
+                out=dx[:],
+                lhsT=w1_sb[:, e * 256 : (e + 1) * 256].bitcast(E2M1),
+                lhsT_scale=w1_sc[:, e * K : (e + 1) * K],
+                rhs=words[:].bitcast(E5M2),
+                rhs_scale=scales[:],
+                start=True,
+                stop=True,
+            )
+            nc.scalar.activation(dx_sb[:, e * C : (e + 1) * C], dx[:], COPY)
+
+        steps = [(0, 0), (1, 0), (0, 1), (1, 1), (0, 2), (1, 2)] + [(e, s) for e in (2, 3) for s in range(PASSES)]
+        todo = {}
+
+        def later(k, work):
+            todo.setdefault(k, []).append(work)
+
+        def after_quantise(e, s, k):
+            if e == 1:
+                if s == PASSES - 1:
+                    for x in range(PASSES):
+                        multiply2(1, x)
+            else:
+                multiply2(e, s)
+            if s == PASSES - 1:
+                empty_dh(e)
+
+        pending = None
+        for k in range(len(steps) + 1):
+            if k < len(steps):
+                e, s = steps[k]
+                for t in range(3):
+                    gather(e, s, t)
+            if pending is not None:
+                pe, ps = pending
+                quantise(pe, ps)
+                after_quantise(pe, ps, k)
+            if k < len(steps):
+                gather(e, s, 3)
+                interleave(e, s)
+                pending = (e, s)
+            if k == 6:
+                slope(0)
+                for q in range(QT):
+                    da_part(0, q)
+            if k == 7:
+                finish(0)
+                slope(1)
+                for q in range(QT):
+                    da_part(1, q)
+            if k == 8:
+                finish(1)
+            if k == 10:
+                slope(2)
+            if k == 11:
+                slope(3)
+        for q in range(QT):
+            da_part(2, q)
+        finish(2)
+        for q in range(QT):
+            da_part(3, q)
+        finish(3)
+
+        nc.vector.tensor_copy(first[:], dx_sb[:].indirect(pos1_sb[:]))
+        for h in range(2):
+            cols = slice(h * (T // 2), (h + 1) * (T // 2))
+            lists = slice(h * (T // 32), (h + 1) * (T // 32))
+            nc.vector.tensor_copy(second[:, cols], dx_sb[:].indirect(pos2_sb[:, lists]))
+            nc.vector.tensor_tensor(total[:, cols], first[:, cols], second[:, cols], ADD)
+            nc.sync.dma_start(out=out[:, cols], in_=total[:, cols])

@@ -34,47 +34,51 @@ def tile_moe_bdx_mlp_relu2_kernel(
     tc, dyT, a, w2_words, w2_scales, w1_words, w1_scales, gate, offs, pos1, pos2, out
 ):
     nc = tc.nc
+    PAIR = 2 * C
     with ExitStack() as ctx:
         keep = ctx.enter_context(tc.tile_pool(name="keep", bufs=1))
-        gathered = ctx.enter_context(tc.tile_pool(name="gathered", bufs=3))
+        gathered = ctx.enter_context(tc.tile_pool(name="gathered", bufs=2))
         grouped = ctx.enter_context(tc.tile_pool(name="grouped", bufs=3))
-        coded = ctx.enter_context(tc.tile_pool(name="coded", bufs=8))
+        coded = ctx.enter_context(tc.tile_pool(name="coded", bufs=4))
         hidden = ctx.enter_context(tc.tile_pool(name="hidden", bufs=8))
         da_pool = ctx.enter_context(tc.tile_pool(name="da_pool", bufs=2))
+        last_da = ctx.enter_context(tc.tile_pool(name="last_da", bufs=1))
+        slope_pool = ctx.enter_context(tc.tile_pool(name="slope_pool", bufs=3))
         dh_psum = ctx.enter_context(tc.psum_pool(name="dh_psum", bufs=1))
-        tr_psum = ctx.enter_context(tc.psum_pool(name="tr_psum", bufs=2))
-        dx_psum = ctx.enter_context(tc.psum_pool(name="dx_psum", bufs=2))
+        tr_psum = ctx.enter_context(tc.psum_pool(name="tr_psum", bufs=3))
+        dx_psum = ctx.enter_context(tc.psum_pool(name="dx_psum", bufs=1))
 
         offs_sb = keep.tile([P, SLOTS // 16], U16, name="offs_sb")
         pos1_sb = keep.tile([P, T // 16], U16, name="pos1_sb")
         pos2_sb = keep.tile([P, T // 16], U16, name="pos2_sb")
-        gates = [keep.tile([P, C], F32, name=f"gate{e}") for e in range(E)]
+        gates = [keep.tile([P, PAIR], F32, name=f"gate{e}") for e in range(2)]
         planes = [
-            [keep.tile([P, T], F32, name=f"dy{s}_{t}") for t in range(PACK)] for s in range(PASSES)
+            [keep.tile([P, T + 8], F32, name=f"dy{s}_{t}") for t in range(PACK)] for s in range(PASSES)
         ]
         w2_sb = [keep.tile([P, PASSES * 1024], U8, name=f"w2_{e}", align_bytes=64) for e in range(E)]
         w2_sc = keep.tile([P, E * PASSES * H], U8, name="w2_sc", align_bytes=64)
         w1_sb = keep.tile([P, E * 256], U8, name="w1_sb", align_bytes=64)
         w1_sc = keep.tile([P, E * K], U8, name="w1_sc", align_bytes=64)
-        a_sb = [keep.tile([P, PACK, C], F32, name=f"a{e}") for e in range(E)]
+        a_sb = {}
         ident = keep.tile([P, P], F32, name="ident")
         dx_sb = keep.tile([P, SLOTS], F32, name="dx_sb")
-        first = keep.tile([P, T], F32, name="first")
-        second = keep.tile([P, T], F32, name="second")
-        total = keep.tile([P, T], F32, name="total")
 
+        for s in range(PASSES):
+            for t in range(PACK):
+                nc.gpsimd.memset(planes[s][t][:, T : T + 8], 0.0)
         nc.gpsimd.memset(w2_sc[:].bitcast(I32), 0)
         nc.gpsimd.memset(w1_sc[:].bitcast(I32), 0)
         make_identity(nc, ident[:])
 
         dy_rows = dyT.rearrange("(s p t) j -> s t p j", p=P, t=PACK)
 
-        def load_pass(s):
-            for t in range(PACK):
-                nc.sync.dma_start(out=planes[s][t][:], in_=dy_rows[s, t])
+        def load_plane(s, t):
+            nc.sync.dma_start(out=planes[s][t][:, 0:T], in_=dy_rows[s, t])
 
         def load_gate(e):
-            nc.sync.dma_start(out=gates[e][:], in_=gate[0:P, e * C : (e + 1) * C])
+            nc.sync.dma_start(
+                out=gates[e // 2][:, (e % 2) * C : (e % 2 + 1) * C], in_=gate[0:P, e * C : (e + 1) * C]
+            )
 
         def load_w2(e):
             nc.sync.dma_start(
@@ -83,6 +87,7 @@ def tile_moe_bdx_mlp_relu2_kernel(
             )
 
         def load_a(e):
+            a_sb[e] = da_pool.tile([P, PACK, C], F32, name="a")
             nc.sync.dma_start(
                 out=a_sb[e][:], in_=a[:, e * C : (e + 1) * C].rearrange("(p t) c -> p t c", t=PACK)
             )
@@ -105,71 +110,72 @@ def tile_moe_bdx_mlp_relu2_kernel(
 
         nc.sync.dma_start(offs_sb[:], offs)
         load_gate(0)
-        load_pass(0)
+        load_plane(0, 0)
         load_gate(1)
+        for t in range(1, PACK):
+            load_plane(0, t)
+        for t in range(PACK):
+            load_plane(1, t)
+        load_gate(2)
+        load_gate(3)
+        for t in range(PACK):
+            load_plane(2, t)
         load_scales()
         load_w2(0)
-        load_pass(1)
+        load_a(0)
         load_w2(1)
-        load_pass(2)
+        load_a(1)
         nc.sync.dma_start(
             out=w1_sb[:].bitcast(I32).rearrange("p (e w) -> p e w", e=E),
             in_=w1_words.bitcast(I32).rearrange("e s p w -> p (e s) w"),
         )
-        load_a(0)
-        load_gate(2)
-        load_gate(3)
-        load_a(1)
         load_w2(2)
         load_w2(3)
-        load_a(2)
-        load_a(3)
         nc.sync.dma_start(pos1_sb[:], pos1)
         nc.sync.dma_start(pos2_sb[:], pos2)
 
-        g32 = {}
         codes = {}
         dh_banks = {}
         dh_out = {}
         slopes = {}
-        da_codes = {}
         da_parts = {}
 
-        def gather(e, s, t):
-            if t == 0:
-                g32[e, s] = gathered.tile([P, PACK, C], F32, name="g32")
+        def gather(g32, s, t, slot0, n):
+            base = slot0 % PAIR
             nc.vector.tensor_tensor(
-                g32[e, s][:, t, :],
-                planes[s][t][:].indirect(offs_sb[:, e * (C // 16) : (e + 1) * (C // 16)]),
-                gates[e][:],
+                g32[:, t, base : base + n] if g32.shape[2] == PAIR else g32[:, t, slot0 % C : slot0 % C + n],
+                planes[s][t][:].indirect(offs_sb[:, slot0 // 16 : (slot0 + n) // 16]),
+                gates[slot0 // PAIR][:, base : base + n],
                 MULT,
             )
 
-        def interleave(e, s):
-            gb = grouped.tile([P, C, PACK], BF16, name="gb", align_bytes=64)
-            g32[e, s, "b"] = gb
-            nc.scalar.activation(
-                gb[:].rearrange("p (c i) t -> p c t i", i=4),
-                g32[e, s][:].rearrange("p t (c i) -> p c t i", i=4),
-                COPY,
-            )
+        def interleave(g32, n):
+            gb = grouped.tile([P, n, PACK], BF16, name="gb", align_bytes=64)
+            for h in range(n // C):
+                cols = slice(h * C, (h + 1) * C)
+                nc.scalar.activation(
+                    gb[:, cols, :].rearrange("p (c i) t -> p c t i", i=4),
+                    g32[:, :, cols].rearrange("p t (c i) -> p c t i", i=4),
+                    COPY,
+                )
+            return gb
 
-        def quantise(e, s):
-            words = coded.tile([P, C], U32, name="g_words", align_bytes=64)
-            scales = coded.tile([P, C], U8, name="g_scales", align_bytes=64)
-            codes[e, s] = (words, scales)
+        def quantise(gb, n):
+            words = coded.tile([P, n], U32, name="g_words", align_bytes=64)
+            scales = coded.tile([P, n], U8, name="g_scales", align_bytes=64)
             nc.vector.quantize_mx(
                 out=words[:].bitcast(E5M2),
                 scales=scales[:],
-                in_=g32[e, s, "b"][:].rearrange("p c t -> p (c t)"),
+                in_=gb[:].rearrange("p c t -> p (c t)"),
             )
+            return words, scales
 
         def multiply2(e, s):
-            words, scales = codes[e, s]
+            words, scales, base = codes[e, s]
             for q in range(QT):
                 if s == 0:
                     dh_banks[e, q] = dh_psum.tile([P, H], F32, name=f"dh{q}")
-                cols = slice(q * P, (q + 1) * P)
+                cols = slice(base + q * P, base + (q + 1) * P)
                 nc.tensor.matmul_mx(
                     out=dh_banks[e, q][:],
                     lhsT=words[:, cols].bitcast(E5M2),
@@ -181,7 +187,7 @@ def tile_moe_bdx_mlp_relu2_kernel(
                 )
 
         def slope(e):
-            slopes[e] = da_pool.tile([P, C, PACK], F32, name="slope")
+            slopes[e] = slope_pool.tile([P, C, PACK], F32, name="slope")
             nc.scalar.activation(
                 slopes[e][:], a_sb[e][:].rearrange("p t c -> p c t"), RELU, scale=2.0
             )
@@ -193,28 +199,44 @@ def tile_moe_bdx_mlp_relu2_kernel(
                     dh_out[e, q][:], dh_banks[e, q][:].rearrange("p (m t) -> p t m", t=PACK), COPY
                 )
 
+        turned = {}
+        das = {}
+
+        def turn(e, q):
+            turned[e, q] = tr_psum.tile([P, PACK, P], F32, name="turned")
+            for t in range(PACK):
+                nc.tensor.transpose(turned[e, q][:, t, :], dh_out[e, q][:, t, :], ident[:])
+
         def da_part(e, q):
             if q == 0:
-                da_parts[e] = da_pool.tile([P, C, PACK], BF16, name="da", align_bytes=64)
-            turned = tr_psum.tile([P, PACK, P], F32, name="turned")
-            for t in range(PACK):
-                nc.tensor.transpose(turned[:, t, :], dh_out[e, q][:, t, :], ident[:])
+                if e == 1:
+                    both = grouped.tile([P, PAIR, PACK], BF16, name="gb", align_bytes=64)
+                    das[1], das[2] = both[:, 0:C, :], both[:, C:PAIR, :]
+                elif e != 2:
+                    das[e] = last_da.tile([P, C, PACK], BF16, name=f"da{e}", align_bytes=64)[:]
+                da_parts[e] = (
+                    das[e],
+                    da_pool.tile([P, C], U32, name="da_words", align_bytes=64),
+                    da_pool.tile([P, C], U8, name="da_scales", align_bytes=64),
+                )
             cols = slice(q * P, (q + 1) * P)
             nc.vector.tensor_tensor(
-                da_parts[e][:, cols, :],
+                da_parts[e][0][:, cols, :],
                 slopes[e][:, cols, :],
-                turned[:].rearrange("p t c -> p c t"),
+                turned[e, q][:].rearrange("p t c -> p c t"),
                 MULT,
             )
 
-        def finish(e):
-            words = da_pool.tile([P, C], U32, name="da_words", align_bytes=64)
-            scales = da_pool.tile([P, C], U8, name="da_scales", align_bytes=64)
+        def quantise_da(e, c0, c1):
+            da, words, scales = da_parts[e]
             nc.vector.quantize_mx(
-                out=words[:].bitcast(E5M2),
-                scales=scales[:],
-                in_=da_parts[e][:].rearrange("p c t -> p (c t)"),
+                out=words[:, c0:c1].bitcast(E5M2),
+                scales=scales[:, c0:c1],
+                in_=da[:, c0:c1, :].rearrange("p c t -> p (c t)"),
             )
+
+        def multiply1(e):
+            da, words, scales = da_parts[e]
             dx = dx_psum.tile([P, C], F32, name="dx")
             nc.tensor.matmul_mx(
                 out=dx[:],
@@ -227,62 +249,133 @@ def tile_moe_bdx_mlp_relu2_kernel(
             )
             nc.scalar.activation(dx_sb[:, e * C : (e + 1) * C], dx[:], COPY)
 
-        steps = [(0, 0), (1, 0), (0, 1), (1, 1), (0, 2), (1, 2)] + [(e, s) for e in (2, 3) for s in range(PASSES)]
-        todo = {}
+        def finish(e):
+            quantise_da(e, 0, C)
+            multiply1(e)
 
-        def later(k, work):
-            todo.setdefault(k, []).append(work)
+        def pair_gathers(pair, s, g32, ts):
+            for t in ts:
+                if pair == 0 and s == 0 and t == 0:
+                    gather(g32, s, t, 0, C)
+                    gather(g32, s, t, C, C)
+                else:
+                    gather(g32, s, t, pair * PAIR, PAIR)
 
-        def after_quantise(e, s, k):
-            if e == 1:
-                if s == PASSES - 1:
-                    for x in range(PASSES):
-                        multiply2(1, x)
-            else:
-                multiply2(e, s)
-            if s == PASSES - 1:
-                empty_dh(e)
+        def pair_tile():
+            return gathered.tile([P, PACK, PAIR], F32, name="g32")
 
-        pending = None
-        for k in range(len(steps) + 1):
-            if k < len(steps):
-                e, s = steps[k]
-                for t in range(3):
-                    gather(e, s, t)
-            if pending is not None:
-                pe, ps = pending
-                quantise(pe, ps)
-                after_quantise(pe, ps, k)
-            if k < len(steps):
-                gather(e, s, 3)
-                interleave(e, s)
-                pending = (e, s)
-            if k == 6:
-                slope(0)
-                for q in range(QT):
-                    da_part(0, q)
-            if k == 7:
-                finish(0)
-                slope(1)
-                for q in range(QT):
-                    da_part(1, q)
-            if k == 8:
-                finish(1)
-            if k == 10:
-                slope(2)
-            if k == 11:
-                slope(3)
+        def pair_codes(gb, pair, s):
+            words, scales = quantise(gb, PAIR)
+            for x in range(2):
+                codes[2 * pair + x, s] = (words, scales, x * C)
+
+        def interleave_half(g32):
+            gb = grouped.tile([P, C, PACK], BF16, name="gb", align_bytes=64)
+            nc.scalar.activation(
+                gb[:].rearrange("p (c i) t -> p c t i", i=4),
+                g32[:].rearrange("p t (c i) -> p c t i", i=4),
+                COPY,
+            )
+            return gb
+
+        g = pair_tile()
+        pair_gathers(0, 0, g, range(4))
+        b = interleave(g, PAIR)
+        for s in (1, 2):
+            g = pair_tile()
+            pair_gathers(0, s, g, range(3))
+            pair_codes(b, 0, s - 1)
+            multiply2(0, s - 1)
+            pair_gathers(0, s, g, range(3, 4))
+            b = interleave(g, PAIR)
+            slope(s - 1)
+            load_a(s + 1)
+        def single(e, s):
+            g1 = gathered.tile([P, PACK, C], F32, name="g32")
+            for t in range(4):
+                gather(g1, s, t, e * C, C)
+            return g1
+
+        def single_codes(e, s, gb):
+            codes[e, s] = quantise(gb, C) + (0,)
+
+        g = pair_tile()
+        pair_gathers(1, 0, g, range(3))
+        pair_codes(b, 0, 2)
+        multiply2(0, 2)
+        empty_dh(0)
+        for q in range(3):
+            turn(0, q)
+        for s in range(PASSES):
+            multiply2(1, s)
+        pair_gathers(1, 0, g, range(3, 4))
+        b = interleave(g, PAIR)
+        empty_dh(1)
+        slope(2)
+        g = single(2, 1)
+        b21 = interleave_half(g)
+        da_part(0, 0)
+        turn(0, 3)
+        for q in range(1, QT):
+            da_part(0, q)
+        slope(3)
+        for q in range(3):
+            turn(1, q)
+        pair_codes(b, 1, 0)
+        multiply2(2, 0)
+        quantise_da(0, 0, C)
+        multiply1(0)
+        g = single(2, 2)
+        b22 = interleave_half(g)
+        single_codes(2, 1, b21)
+        multiply2(2, 1)
+        g = single(3, 1)
+        b31 = interleave_half(g)
+        single_codes(2, 2, b22)
+        multiply2(2, 2)
+        empty_dh(2)
+        multiply2(3, 0)
+        g = single(3, 2)
+        b32 = interleave_half(g)
+        single_codes(3, 1, b31)
+        multiply2(3, 1)
+        da_part(1, 0)
+        turn(1, 3)
+        for q in range(1, QT):
+            da_part(1, q)
+            turn(2, q - 1)
+        quantise_da(1, 0, C)
+        multiply1(1)
+        single_codes(3, 2, b32)
+        multiply2(3, 2)
+        empty_dh(3)
         for q in range(QT):
             da_part(2, q)
-        finish(2)
+            if q == 0:
+                turn(2, 3)
+            if q > 0:
+                turn(3, q - 1)
+        quantise_da(2, 0, C)
+        multiply1(2)
         for q in range(QT):
             da_part(3, q)
-        finish(3)
+            if q == 0:
+                turn(3, 3)
+            if q == 2:
+                quantise_da(3, 0, C // 2)
+        quantise_da(3, C // 2, C)
+        multiply1(3)
 
+        first = da_pool.tile([P, T], F32, name="a")
+        second = da_pool.tile([P, T], F32, name="a")
+        total = slope_pool.tile([P, T], F32, name="slope")
         nc.vector.tensor_copy(first[:], dx_sb[:].indirect(pos1_sb[:]))
-        for h in range(2):
-            cols = slice(h * (T // 2), (h + 1) * (T // 2))
-            lists = slice(h * (T // 32), (h + 1) * (T // 32))
-            nc.vector.tensor_copy(second[:, cols], dx_sb[:].indirect(pos2_sb[:, lists]))
-            nc.vector.tensor_tensor(total[:, cols], first[:, cols], second[:, cols], ADD)
+        lo = 0
+        for width, adder in ((640, nc.gpsimd), (384, nc.vector)):
+            cols = slice(lo, lo + width)
+            nc.vector.tensor_copy(
+                second[:, cols], dx_sb[:].indirect(pos2_sb[:, lo // 16 : (lo + width) // 16])
+            )
+            adder.tensor_tensor(total[:, cols], first[:, cols], second[:, cols], ADD)
             nc.sync.dma_start(out=out[:, cols], in_=total[:, cols])
+            lo += width

@@ -38,15 +38,14 @@ def tile_moe_bdx_mlp_relu2_kernel(
     with ExitStack() as ctx:
         keep = ctx.enter_context(tc.tile_pool(name="keep", bufs=1))
         gathered = ctx.enter_context(tc.tile_pool(name="gathered", bufs=2))
-        grouped = ctx.enter_context(tc.tile_pool(name="grouped", bufs=3))
+        grouped = ctx.enter_context(tc.tile_pool(name="grouped", bufs=2))
         coded = ctx.enter_context(tc.tile_pool(name="coded", bufs=4))
         hidden = ctx.enter_context(tc.tile_pool(name="hidden", bufs=8))
-        da_pool = ctx.enter_context(tc.tile_pool(name="da_pool", bufs=2))
+        a_pool = ctx.enter_context(tc.tile_pool(name="a_pool", bufs=2))
         last_da = ctx.enter_context(tc.tile_pool(name="last_da", bufs=1))
-        slope_pool = ctx.enter_context(tc.tile_pool(name="slope_pool", bufs=3))
+        slope_pool = ctx.enter_context(tc.tile_pool(name="slope_pool", bufs=4))
         dh_psum = ctx.enter_context(tc.psum_pool(name="dh_psum", bufs=1))
-        tr_psum = ctx.enter_context(tc.psum_pool(name="tr_psum", bufs=3))
-        dx_psum = ctx.enter_context(tc.psum_pool(name="dx_psum", bufs=1))
+        tr_psum = ctx.enter_context(tc.psum_pool(name="tr_psum", bufs=4))
 
         offs_sb = keep.tile([P, SLOTS // 16], U16, name="offs_sb")
         pos1_sb = keep.tile([P, T // 16], U16, name="pos1_sb")
@@ -87,7 +86,7 @@ def tile_moe_bdx_mlp_relu2_kernel(
             )
 
         def load_a(e):
-            a_sb[e] = da_pool.tile([P, PACK, C], F32, name="a")
+            a_sb[e] = a_pool.tile([P, PACK, C], F32, name="a")
             nc.sync.dma_start(
                 out=a_sb[e][:], in_=a[:, e * C : (e + 1) * C].rearrange("(p t) c -> p t c", t=PACK)
             )
@@ -114,26 +113,14 @@ def tile_moe_bdx_mlp_relu2_kernel(
         load_gate(1)
         for t in range(1, PACK):
             load_plane(0, t)
+        load_a(0)
         for t in range(PACK):
             load_plane(1, t)
-        load_gate(2)
-        load_gate(3)
         for t in range(PACK):
             load_plane(2, t)
-        load_scales()
-        load_w2(0)
-        load_a(0)
-        load_w2(1)
         load_a(1)
-        nc.sync.dma_start(
-            out=w1_sb[:].bitcast(I32).rearrange("p (e w) -> p e w", e=E),
-            in_=w1_words.bitcast(I32).rearrange("e s p w -> p (e s) w"),
-        )
-        load_w2(2)
-        load_w2(3)
-        nc.sync.dma_start(pos1_sb[:], pos1)
-        nc.sync.dma_start(pos2_sb[:], pos2)
-
+        load_gate(2)
+        load_gate(3)
         codes = {}
         dh_banks = {}
         dh_out = {}
@@ -151,13 +138,11 @@ def tile_moe_bdx_mlp_relu2_kernel(
 
         def interleave(g32, n):
             gb = grouped.tile([P, n, PACK], BF16, name="gb", align_bytes=64)
-            for h in range(n // C):
-                cols = slice(h * C, (h + 1) * C)
-                nc.scalar.activation(
-                    gb[:, cols, :].rearrange("p (c i) t -> p c t i", i=4),
-                    g32[:, :, cols].rearrange("p t (c i) -> p c t i", i=4),
-                    COPY,
-                )
+            nc.scalar.activation(
+                gb[:].rearrange("p (c i) t -> p c t i", i=4),
+                g32[:].rearrange("p t (c i) -> p c t i", i=4),
+                COPY,
+            )
             return gb
 
         def quantise(gb, n):
@@ -200,7 +185,6 @@ def tile_moe_bdx_mlp_relu2_kernel(
                 )
 
         turned = {}
-        das = {}
 
         def turn(e, q):
             turned[e, q] = tr_psum.tile([P, PACK, P], F32, name="turned")
@@ -209,26 +193,24 @@ def tile_moe_bdx_mlp_relu2_kernel(
 
         def da_part(e, q):
             if q == 0:
-                if e == 1:
-                    both = grouped.tile([P, PAIR, PACK], BF16, name="gb", align_bytes=64)
-                    das[1], das[2] = both[:, 0:C, :], both[:, C:PAIR, :]
-                elif e != 2:
-                    das[e] = last_da.tile([P, C, PACK], BF16, name=f"da{e}", align_bytes=64)[:]
-                da_parts[e] = (
-                    das[e],
-                    da_pool.tile([P, C], U32, name="da_words", align_bytes=64),
-                    da_pool.tile([P, C], U8, name="da_scales", align_bytes=64),
-                )
+                if e in (0, 3):
+                    da_parts[e] = (
+                        (grouped if e == 0 else last_da).tile([P, C, PACK], BF16, name="gb" if e == 0 else "da3", align_bytes=64),
+                        last_da.tile([P, C], U32, name=f"da_words{e}", align_bytes=64),
+                        last_da.tile([P, C], U8, name=f"da_scales{e}", align_bytes=64),
+                        0,
+                    )
             cols = slice(q * P, (q + 1) * P)
+            base = da_parts[e][3]
             nc.vector.tensor_tensor(
-                da_parts[e][0][:, cols, :],
+                da_parts[e][0][:, base + q * P : base + (q + 1) * P, :],
                 slopes[e][:, cols, :],
                 turned[e, q][:].rearrange("p t c -> p c t"),
                 MULT,
             )
 
         def quantise_da(e, c0, c1):
-            da, words, scales = da_parts[e]
+            da, words, scales, base = da_parts[e]
             nc.vector.quantize_mx(
                 out=words[:, c0:c1].bitcast(E5M2),
                 scales=scales[:, c0:c1],
@@ -236,14 +218,14 @@ def tile_moe_bdx_mlp_relu2_kernel(
             )
 
         def multiply1(e):
-            da, words, scales = da_parts[e]
-            dx = dx_psum.tile([P, C], F32, name="dx")
+            da, words, scales, base = da_parts[e]
+            dx = tr_psum.tile([P, C], F32, name="turned")
             nc.tensor.matmul_mx(
                 out=dx[:],
                 lhsT=w1_sb[:, e * 256 : (e + 1) * 256].bitcast(E2M1),
                 lhsT_scale=w1_sc[:, e * K : (e + 1) * K],
-                rhs=words[:].bitcast(E5M2),
-                rhs_scale=scales[:],
+                rhs=words[:, base : base + C].bitcast(E5M2),
+                rhs_scale=scales[:, base : base + C],
                 start=True,
                 stop=True,
             )
@@ -281,6 +263,11 @@ def tile_moe_bdx_mlp_relu2_kernel(
         g = pair_tile()
         pair_gathers(0, 0, g, range(4))
         b = interleave(g, PAIR)
+        slope(0)
+        load_a(2)
+        load_scales()
+        load_w2(0)
+        load_w2(1)
         for s in (1, 2):
             g = pair_tile()
             pair_gathers(0, s, g, range(3))
@@ -288,8 +275,17 @@ def tile_moe_bdx_mlp_relu2_kernel(
             multiply2(0, s - 1)
             pair_gathers(0, s, g, range(3, 4))
             b = interleave(g, PAIR)
-            slope(s - 1)
-            load_a(s + 1)
+            if s == 1:
+                slope(1)
+                load_a(3)
+                nc.sync.dma_start(
+                    out=w1_sb[:].bitcast(I32).rearrange("p (e w) -> p e w", e=E),
+                    in_=w1_words.bitcast(I32).rearrange("e s p w -> p (e s) w"),
+                )
+                load_w2(2)
+                load_w2(3)
+                nc.sync.dma_start(pos1_sb[:], pos1)
+                nc.sync.dma_start(pos2_sb[:], pos2)
         def single(e, s):
             g1 = gathered.tile([P, PACK, C], F32, name="g32")
             for t in range(4):
@@ -300,35 +296,31 @@ def tile_moe_bdx_mlp_relu2_kernel(
             codes[e, s] = quantise(gb, C) + (0,)
 
         g = pair_tile()
-        pair_gathers(1, 0, g, range(3))
+        slope(2)
+        pair_gathers(1, 0, g, range(4))
+        b_next = interleave(g, PAIR)
         pair_codes(b, 0, 2)
+        b = b_next
         multiply2(0, 2)
         empty_dh(0)
-        for q in range(3):
+        for q in range(QT):
             turn(0, q)
         for s in range(PASSES):
             multiply2(1, s)
-        pair_gathers(1, 0, g, range(3, 4))
-        b = interleave(g, PAIR)
-        empty_dh(1)
-        slope(2)
+        slope(3)
         g = single(2, 1)
         b21 = interleave_half(g)
-        da_part(0, 0)
-        turn(0, 3)
-        for q in range(1, QT):
-            da_part(0, q)
-        slope(3)
-        for q in range(3):
-            turn(1, q)
+        empty_dh(1)
+        g = single(2, 2)
         pair_codes(b, 1, 0)
         multiply2(2, 0)
-        quantise_da(0, 0, C)
-        multiply1(0)
-        g = single(2, 2)
+        for q in range(QT):
+            da_part(0, q)
+            turn(1, q)
         b22 = interleave_half(g)
         single_codes(2, 1, b21)
         multiply2(2, 1)
+        quantise_da(0, 0, C)
         g = single(3, 1)
         b31 = interleave_half(g)
         single_codes(2, 2, b22)
@@ -337,37 +329,39 @@ def tile_moe_bdx_mlp_relu2_kernel(
         multiply2(3, 0)
         g = single(3, 2)
         b32 = interleave_half(g)
+        both = (
+            grouped.tile([P, PAIR, PACK], BF16, name="gb", align_bytes=64),
+            coded.tile([P, PAIR], U32, name="g_words", align_bytes=64),
+            coded.tile([P, PAIR], U8, name="g_scales", align_bytes=64),
+        )
+        da_parts[1] = both + (0,)
+        da_parts[2] = both + (C,)
         single_codes(3, 1, b31)
         multiply2(3, 1)
-        da_part(1, 0)
-        turn(1, 3)
-        for q in range(1, QT):
+        for q in range(QT):
             da_part(1, q)
-            turn(2, q - 1)
-        quantise_da(1, 0, C)
-        multiply1(1)
+            turn(2, q)
         single_codes(3, 2, b32)
+        multiply1(0)
         multiply2(3, 2)
         empty_dh(3)
         for q in range(QT):
             da_part(2, q)
-            if q == 0:
-                turn(2, 3)
-            if q > 0:
-                turn(3, q - 1)
-        quantise_da(2, 0, C)
+            if q < 3:
+                turn(3, q)
+        quantise_da(1, 0, PAIR)
+        turn(3, 3)
+        multiply1(1)
         multiply1(2)
         for q in range(QT):
             da_part(3, q)
-            if q == 0:
-                turn(3, 3)
             if q == 2:
                 quantise_da(3, 0, C // 2)
         quantise_da(3, C // 2, C)
         multiply1(3)
 
-        first = da_pool.tile([P, T], F32, name="a")
-        second = da_pool.tile([P, T], F32, name="a")
+        first = slope_pool.tile([P, T], F32, name="slope")
+        second = slope_pool.tile([P, T], F32, name="slope")
         total = slope_pool.tile([P, T], F32, name="slope")
         nc.vector.tensor_copy(first[:], dx_sb[:].indirect(pos1_sb[:]))
         lo = 0

@@ -38,12 +38,13 @@ def tile_moe_bdx_mlp_relu2_kernel(
     with ExitStack() as ctx:
         keep = ctx.enter_context(tc.tile_pool(name="keep", bufs=1))
         gathered = ctx.enter_context(tc.tile_pool(name="gathered", bufs=2))
-        grouped = ctx.enter_context(tc.tile_pool(name="grouped", bufs=2))
+        grouped = ctx.enter_context(tc.tile_pool(name="grouped", bufs=3))
         coded = ctx.enter_context(tc.tile_pool(name="coded", bufs=4))
         hidden = ctx.enter_context(tc.tile_pool(name="hidden", bufs=8))
         a_pool = ctx.enter_context(tc.tile_pool(name="a_pool", bufs=2))
         last_da = ctx.enter_context(tc.tile_pool(name="last_da", bufs=1))
-        slope_pool = ctx.enter_context(tc.tile_pool(name="slope_pool", bufs=4))
+        da_codes_pool = ctx.enter_context(tc.tile_pool(name="da_codes_pool", bufs=3))
+        slope_pool = ctx.enter_context(tc.tile_pool(name="slope_pool", bufs=3))
         dh_psum = ctx.enter_context(tc.psum_pool(name="dh_psum", bufs=1))
         tr_psum = ctx.enter_context(tc.psum_pool(name="tr_psum", bufs=4))
 
@@ -64,7 +65,7 @@ def tile_moe_bdx_mlp_relu2_kernel(
 
         for s in range(PASSES):
             for t in range(PACK):
-                nc.gpsimd.memset(planes[s][t][:, T : T + 8], 0.0)
+                nc.vector.memset(planes[s][t][:, T : T + 8], 0.0)
         nc.gpsimd.memset(w2_sc[:].bitcast(I32), 0)
         nc.gpsimd.memset(w1_sc[:].bitcast(I32), 0)
         make_identity(nc, ident[:])
@@ -113,12 +114,15 @@ def tile_moe_bdx_mlp_relu2_kernel(
         load_gate(1)
         for t in range(1, PACK):
             load_plane(0, t)
-        load_a(0)
-        for t in range(PACK):
+        for t in range(3):
             load_plane(1, t)
-        for t in range(PACK):
-            load_plane(2, t)
+        load_a(0)
+        load_plane(1, 3)
+        load_plane(2, 0)
+        load_plane(2, 1)
+        load_plane(2, 2)
         load_a(1)
+        load_plane(2, 3)
         load_gate(2)
         load_gate(3)
         codes = {}
@@ -129,8 +133,9 @@ def tile_moe_bdx_mlp_relu2_kernel(
 
         def gather(g32, s, t, slot0, n):
             base = slot0 % PAIR
+            here = slot0 % g32.shape[2]
             nc.vector.tensor_tensor(
-                g32[:, t, base : base + n] if g32.shape[2] == PAIR else g32[:, t, slot0 % C : slot0 % C + n],
+                g32[:, t, here : here + n],
                 planes[s][t][:].indirect(offs_sb[:, slot0 // 16 : (slot0 + n) // 16]),
                 gates[slot0 // PAIR][:, base : base + n],
                 MULT,
@@ -155,9 +160,9 @@ def tile_moe_bdx_mlp_relu2_kernel(
             )
             return words, scales
 
-        def multiply2(e, s):
+        def multiply2(e, s, qs=range(QT)):
             words, scales, base = codes[e, s]
-            for q in range(QT):
+            for q in qs:
                 if s == 0:
                     dh_banks[e, q] = dh_psum.tile([P, H], F32, name=f"dh{q}")
                 cols = slice(base + q * P, base + (q + 1) * P)
@@ -177,8 +182,8 @@ def tile_moe_bdx_mlp_relu2_kernel(
                 slopes[e][:], a_sb[e][:].rearrange("p t c -> p c t"), RELU, scale=2.0
             )
 
-        def empty_dh(e):
-            for q in range(QT):
+        def empty_dh(e, qs=range(QT)):
+            for q in qs:
                 dh_out[e, q] = hidden.tile([P, PACK, P], F32, name="dh_out")
                 nc.scalar.activation(
                     dh_out[e, q][:], dh_banks[e, q][:].rearrange("p (m t) -> p t m", t=PACK), COPY
@@ -191,15 +196,17 @@ def tile_moe_bdx_mlp_relu2_kernel(
             for t in range(PACK):
                 nc.tensor.transpose(turned[e, q][:, t, :], dh_out[e, q][:, t, :], ident[:])
 
+        def make_da(e):
+            da_parts[e] = (
+                (last_da if e == 3 else grouped).tile([P, C, PACK], BF16, name="da" if e == 3 else "gb", align_bytes=64),
+                da_codes_pool.tile([P, C], U32, name="da_words", align_bytes=64),
+                da_codes_pool.tile([P, C], U8, name="da_scales", align_bytes=64),
+                0,
+            )
+
         def da_part(e, q):
-            if q == 0:
-                if e in (0, 3):
-                    da_parts[e] = (
-                        (grouped if e == 0 else last_da).tile([P, C, PACK], BF16, name="gb" if e == 0 else "da3", align_bytes=64),
-                        last_da.tile([P, C], U32, name=f"da_words{e}", align_bytes=64),
-                        last_da.tile([P, C], U8, name=f"da_scales{e}", align_bytes=64),
-                        0,
-                    )
+            if e not in da_parts:
+                make_da(e)
             cols = slice(q * P, (q + 1) * P)
             base = da_parts[e][3]
             nc.vector.tensor_tensor(
@@ -307,56 +314,89 @@ def tile_moe_bdx_mlp_relu2_kernel(
             turn(0, q)
         for s in range(PASSES):
             multiply2(1, s)
-        slope(3)
         g = single(2, 1)
         b21 = interleave_half(g)
         empty_dh(1)
         g = single(2, 2)
+        b22 = interleave_half(g)
         pair_codes(b, 1, 0)
         multiply2(2, 0)
         for q in range(QT):
             da_part(0, q)
             turn(1, q)
-        b22 = interleave_half(g)
+        slope(3)
         single_codes(2, 1, b21)
         multiply2(2, 1)
         quantise_da(0, 0, C)
         g = single(3, 1)
-        b31 = interleave_half(g)
         single_codes(2, 2, b22)
         multiply2(2, 2)
+        b31 = interleave_half(g)
         empty_dh(2)
         multiply2(3, 0)
-        g = single(3, 2)
-        b32 = interleave_half(g)
-        both = (
-            grouped.tile([P, PAIR, PACK], BF16, name="gb", align_bytes=64),
-            coded.tile([P, PAIR], U32, name="g_words", align_bytes=64),
-            coded.tile([P, PAIR], U8, name="g_scales", align_bytes=64),
-        )
-        da_parts[1] = both + (0,)
-        da_parts[2] = both + (C,)
-        single_codes(3, 1, b31)
-        multiply2(3, 1)
         for q in range(QT):
             da_part(1, q)
-            turn(2, q)
-        single_codes(3, 2, b32)
+        quantise_da(1, 0, C)
         multiply1(0)
-        multiply2(3, 2)
-        empty_dh(3)
+        HALF = C // 2
+        b32 = grouped.tile([P, C, PACK], BF16, name="gb", align_bytes=64)
+        words32 = coded.tile([P, C], U32, name="g_words", align_bytes=64)
+        scales32 = coded.tile([P, C], U8, name="g_scales", align_bytes=64)
+        codes[3, 2] = (words32, scales32, 0)
+
+        def last_gather(h):
+            if h == 0:
+                g1 = gathered.tile([P, PACK, HALF], F32, name="g32")
+            else:
+                g1 = grouped.tile([P, PACK, HALF], F32, name="gb", align_bytes=64)
+            for t in range(4):
+                gather(g1, 2, t, 3 * C + h * HALF, HALF)
+            return g1
+
+        def last_interleave(g1, h):
+            nc.scalar.activation(
+                b32[:, h * HALF : (h + 1) * HALF, :].rearrange("p (c i) t -> p c t i", i=4),
+                g1[:].rearrange("p t (c i) -> p c t i", i=4),
+                COPY,
+            )
+
+        def last_quantise(h):
+            cols = slice(h * HALF, (h + 1) * HALF)
+            nc.vector.quantize_mx(
+                out=words32[:, cols].bitcast(E5M2),
+                scales=scales32[:, cols],
+                in_=b32[:, cols, :].rearrange("p c t -> p (c t)"),
+            )
+
         for q in range(QT):
+            turn(2, q)
+        g = last_gather(0)
+        last_interleave(g, 0)
+        single_codes(3, 1, b31)
+        multiply2(3, 1)
+        make_da(2)
+        g = last_gather(1)
+        last_quantise(0)
+        multiply2(3, 2, range(2))
+        last_interleave(g, 1)
+        empty_dh(3, range(2))
+        for q in range(2):
             da_part(2, q)
-            if q < 3:
-                turn(3, q)
-        quantise_da(1, 0, PAIR)
-        turn(3, 3)
+            turn(3, q)
+        last_quantise(1)
+        multiply2(3, 2, range(2, 4))
+        empty_dh(3, range(2, 4))
+        for q in range(2, 4):
+            da_part(2, q)
+            turn(3, q)
+        da_part(3, 0)
+        da_part(3, 1)
+        quantise_da(2, 0, C)
         multiply1(1)
         multiply1(2)
-        for q in range(QT):
-            da_part(3, q)
-            if q == 2:
-                quantise_da(3, 0, C // 2)
+        da_part(3, 2)
+        quantise_da(3, 0, C // 2)
+        da_part(3, 3)
         quantise_da(3, C // 2, C)
         multiply1(3)
 

@@ -38,15 +38,15 @@ def tile_moe_bdx_mlp_relu2_kernel(
     with ExitStack() as ctx:
         keep = ctx.enter_context(tc.tile_pool(name="keep", bufs=1))
         gathered = ctx.enter_context(tc.tile_pool(name="gathered", bufs=2))
-        grouped = ctx.enter_context(tc.tile_pool(name="grouped", bufs=3))
+        grouped = ctx.enter_context(tc.tile_pool(name="grouped", bufs=2))
         coded = ctx.enter_context(tc.tile_pool(name="coded", bufs=4))
-        hidden = ctx.enter_context(tc.tile_pool(name="hidden", bufs=8))
+        hidden = ctx.enter_context(tc.tile_pool(name="hidden", bufs=4))
         a_pool = ctx.enter_context(tc.tile_pool(name="a_pool", bufs=2))
-        last_da = ctx.enter_context(tc.tile_pool(name="last_da", bufs=1))
+        last_da = ctx.enter_context(tc.tile_pool(name="last_da", bufs=2))
         da_codes_pool = ctx.enter_context(tc.tile_pool(name="da_codes_pool", bufs=3))
-        slope_pool = ctx.enter_context(tc.tile_pool(name="slope_pool", bufs=3))
-        dh_psum = ctx.enter_context(tc.psum_pool(name="dh_psum", bufs=1))
-        tr_psum = ctx.enter_context(tc.psum_pool(name="tr_psum", bufs=4))
+        slope_pool = ctx.enter_context(tc.tile_pool(name="slope_pool", bufs=4))
+        dh_psum = ctx.enter_context(tc.psum_pool(name="dh_psum", bufs=5))
+        tr_psum = ctx.enter_context(tc.psum_pool(name="tr_psum", bufs=3))
 
         offs_sb = keep.tile([P, SLOTS // 16], U16, name="offs_sb")
         pos1_sb = keep.tile([P, T // 16], U16, name="pos1_sb")
@@ -61,6 +61,7 @@ def tile_moe_bdx_mlp_relu2_kernel(
         w1_sc = keep.tile([P, E * K], U8, name="w1_sc", align_bytes=64)
         a_sb = {}
         ident = keep.tile([P, P], F32, name="ident")
+        ident_bf = keep.tile([P, P], BF16, name="ident_bf")
         dx_sb = keep.tile([P, SLOTS], F32, name="dx_sb")
 
         for s in range(PASSES):
@@ -69,6 +70,7 @@ def tile_moe_bdx_mlp_relu2_kernel(
         nc.gpsimd.memset(w2_sc[:].bitcast(I32), 0)
         nc.gpsimd.memset(w1_sc[:].bitcast(I32), 0)
         make_identity(nc, ident[:])
+        make_identity(nc, ident_bf[:])
 
         dy_rows = dyT.rearrange("(s p t) j -> s t p j", p=P, t=PACK)
 
@@ -114,20 +116,17 @@ def tile_moe_bdx_mlp_relu2_kernel(
         load_gate(1)
         for t in range(1, PACK):
             load_plane(0, t)
-        for t in range(3):
-            load_plane(1, t)
         load_a(0)
-        load_plane(1, 3)
-        load_plane(2, 0)
-        load_plane(2, 1)
-        load_plane(2, 2)
+        for t in range(PACK):
+            load_plane(1, t)
         load_a(1)
-        load_plane(2, 3)
         load_gate(2)
         load_gate(3)
+        for t in range(PACK):
+            load_plane(2, t)
+
         codes = {}
         dh_banks = {}
-        dh_out = {}
         slopes = {}
         da_parts = {}
 
@@ -164,7 +163,7 @@ def tile_moe_bdx_mlp_relu2_kernel(
             words, scales, base = codes[e, s]
             for q in qs:
                 if s == 0:
-                    dh_banks[e, q] = dh_psum.tile([P, H], F32, name=f"dh{q}")
+                    dh_banks[e, q] = dh_psum.tile([P, H], F32, name="dh")
                 cols = slice(base + q * P, base + (q + 1) * P)
                 nc.tensor.matmul_mx(
                     out=dh_banks[e, q][:],
@@ -177,44 +176,42 @@ def tile_moe_bdx_mlp_relu2_kernel(
                 )
 
         def slope(e):
-            slopes[e] = slope_pool.tile([P, C, PACK], F32, name="slope")
-            nc.scalar.activation(
-                slopes[e][:], a_sb[e][:].rearrange("p t c -> p c t"), RELU, scale=2.0
-            )
+            slopes[e] = slope_pool.tile([P, QT, PACK, P], F32, name="slope")
+            for q in range(QT):
+                bank = tr_psum.tile([P, PACK, P], F32, name="turned")
+                for t in range(PACK):
+                    nc.tensor.transpose(bank[:, t, :], a_sb[e][:, t, q * P : (q + 1) * P], ident[:])
+                nc.scalar.activation(slopes[e][:, q, :, :], bank[:], RELU, scale=2.0)
 
-        def empty_dh(e, qs=range(QT)):
-            for q in qs:
-                dh_out[e, q] = hidden.tile([P, PACK, P], F32, name="dh_out")
-                nc.scalar.activation(
-                    dh_out[e, q][:], dh_banks[e, q][:].rearrange("p (m t) -> p t m", t=PACK), COPY
-                )
-
-        turned = {}
-
-        def turn(e, q):
-            turned[e, q] = tr_psum.tile([P, PACK, P], F32, name="turned")
-            for t in range(PACK):
-                nc.tensor.transpose(turned[e, q][:, t, :], dh_out[e, q][:, t, :], ident[:])
+        by_slot = {}
 
         def make_da(e):
             da_parts[e] = (
-                (last_da if e == 3 else grouped).tile([P, C, PACK], BF16, name="da" if e == 3 else "gb", align_bytes=64),
+                last_da.tile([P, C, PACK], BF16, name="da", align_bytes=64),
                 da_codes_pool.tile([P, C], U32, name="da_words", align_bytes=64),
                 da_codes_pool.tile([P, C], U8, name="da_scales", align_bytes=64),
                 0,
             )
 
-        def da_part(e, q):
-            if e not in da_parts:
-                make_da(e)
-            cols = slice(q * P, (q + 1) * P)
-            base = da_parts[e][3]
+        def times(e, q):
+            if e == 2 and q >= 2:
+                by_slot[e, q] = grouped.tile([P, PACK, P], BF16, name="gb", align_bytes=64)
+            else:
+                by_slot[e, q] = hidden.tile([P, PACK, P], BF16, name="by_slot")
             nc.vector.tensor_tensor(
-                da_parts[e][0][:, base + q * P : base + (q + 1) * P, :],
-                slopes[e][:, cols, :],
-                turned[e, q][:].rearrange("p t c -> p c t"),
+                by_slot[e, q][:],
+                dh_banks[e, q][:].rearrange("p (m t) -> p t m", t=PACK),
+                slopes[e][:, q, :, :],
                 MULT,
             )
+
+        def turn(e, q, copy):
+            if e not in da_parts:
+                make_da(e)
+            bank = tr_psum.tile([P, PACK, P], BF16, name="turned")
+            for t in range(PACK):
+                nc.tensor.transpose(bank[:, t, :], by_slot[e, q][:, t, :], ident_bf[:])
+            copy(da_parts[e][0][:, q * P : (q + 1) * P, :], bank[:].rearrange("p t c -> p c t"))
 
         def quantise_da(e, c0, c1):
             da, words, scales, base = da_parts[e]
@@ -275,6 +272,14 @@ def tile_moe_bdx_mlp_relu2_kernel(
         load_scales()
         load_w2(0)
         load_w2(1)
+        nc.sync.dma_start(
+            out=w1_sb[:].bitcast(I32).rearrange("p (e w) -> p e w", e=E),
+            in_=w1_words.bitcast(I32).rearrange("e s p w -> p (e s) w"),
+        )
+        load_w2(2)
+        load_w2(3)
+        nc.sync.dma_start(pos1_sb[:], pos1)
+        nc.sync.dma_start(pos2_sb[:], pos2)
         for s in (1, 2):
             g = pair_tile()
             pair_gathers(0, s, g, range(3))
@@ -282,17 +287,9 @@ def tile_moe_bdx_mlp_relu2_kernel(
             multiply2(0, s - 1)
             pair_gathers(0, s, g, range(3, 4))
             b = interleave(g, PAIR)
+            slope(s)
             if s == 1:
-                slope(1)
                 load_a(3)
-                nc.sync.dma_start(
-                    out=w1_sb[:].bitcast(I32).rearrange("p (e w) -> p e w", e=E),
-                    in_=w1_words.bitcast(I32).rearrange("e s p w -> p (e s) w"),
-                )
-                load_w2(2)
-                load_w2(3)
-                nc.sync.dma_start(pos1_sb[:], pos1)
-                nc.sync.dma_start(pos2_sb[:], pos2)
         def single(e, s):
             g1 = gathered.tile([P, PACK, C], F32, name="g32")
             for t in range(4):
@@ -303,43 +300,47 @@ def tile_moe_bdx_mlp_relu2_kernel(
             codes[e, s] = quantise(gb, C) + (0,)
 
         g = pair_tile()
-        slope(2)
         pair_gathers(1, 0, g, range(4))
         b_next = interleave(g, PAIR)
         pair_codes(b, 0, 2)
         b = b_next
         multiply2(0, 2)
-        empty_dh(0)
         for q in range(QT):
-            turn(0, q)
-        for s in range(PASSES):
-            multiply2(1, s)
+            times(0, q)
+        for q in range(QT):
+            for s in range(PASSES):
+                multiply2(1, s, (q,))
+            turn(0, q, nc.scalar.copy)
+        slope(3)
         g = single(2, 1)
         b21 = interleave_half(g)
-        empty_dh(1)
-        g = single(2, 2)
-        b22 = interleave_half(g)
+        for q in range(QT):
+            times(1, q)
         pair_codes(b, 1, 0)
         multiply2(2, 0)
         for q in range(QT):
-            da_part(0, q)
-            turn(1, q)
-        slope(3)
+            turn(1, q, nc.scalar.copy)
+        quantise_da(0, 0, C)
+        multiply1(0)
+        g = single(2, 2)
+        b22 = interleave_half(g)
         single_codes(2, 1, b21)
         multiply2(2, 1)
-        quantise_da(0, 0, C)
+        quantise_da(1, 0, C)
+        multiply1(1)
         g = single(3, 1)
         single_codes(2, 2, b22)
         multiply2(2, 2)
         b31 = interleave_half(g)
-        empty_dh(2)
-        multiply2(3, 0)
-        for q in range(QT):
-            da_part(1, q)
-        quantise_da(1, 0, C)
-        multiply1(0)
+        for q in range(2):
+            times(2, q)
+            turn(2, q, nc.scalar.copy)
+        multiply2(3, 0, range(2))
         HALF = C // 2
-        b32 = grouped.tile([P, C, PACK], BF16, name="gb", align_bytes=64)
+        b32 = [
+            grouped.tile([P, HALF, PACK], BF16, name="gb", align_bytes=64),
+            hidden.tile([P, HALF, PACK], BF16, name="b32_late", align_bytes=64),
+        ]
         words32 = coded.tile([P, C], U32, name="g_words", align_bytes=64)
         scales32 = coded.tile([P, C], U8, name="g_scales", align_bytes=64)
         codes[3, 2] = (words32, scales32, 0)
@@ -355,7 +356,7 @@ def tile_moe_bdx_mlp_relu2_kernel(
 
         def last_interleave(g1, h):
             nc.scalar.activation(
-                b32[:, h * HALF : (h + 1) * HALF, :].rearrange("p (c i) t -> p c t i", i=4),
+                b32[h][:].rearrange("p (c i) t -> p c t i", i=4),
                 g1[:].rearrange("p t (c i) -> p c t i", i=4),
                 COPY,
             )
@@ -365,38 +366,38 @@ def tile_moe_bdx_mlp_relu2_kernel(
             nc.vector.quantize_mx(
                 out=words32[:, cols].bitcast(E5M2),
                 scales=scales32[:, cols],
-                in_=b32[:, cols, :].rearrange("p c t -> p (c t)"),
+                in_=b32[h][:].rearrange("p c t -> p (c t)"),
             )
 
-        for q in range(QT):
-            turn(2, q)
         g = last_gather(0)
         last_interleave(g, 0)
         single_codes(3, 1, b31)
-        multiply2(3, 1)
-        make_da(2)
+        multiply2(3, 1, range(2))
         g = last_gather(1)
         last_quantise(0)
         multiply2(3, 2, range(2))
         last_interleave(g, 1)
-        empty_dh(3, range(2))
+        times(2, 2)
+        turn(2, 2, nc.scalar.copy)
         for q in range(2):
-            da_part(2, q)
-            turn(3, q)
+            times(3, q)
+            turn(3, q, nc.scalar.copy)
+        multiply2(3, 0, (2,))
+        multiply2(3, 1, (2,))
         last_quantise(1)
-        multiply2(3, 2, range(2, 4))
-        empty_dh(3, range(2, 4))
-        for q in range(2, 4):
-            da_part(2, q)
-            turn(3, q)
-        da_part(3, 0)
-        da_part(3, 1)
+        multiply2(3, 2, (2,))
+        times(2, 3)
+        turn(2, 3, nc.scalar.copy)
+        multiply2(3, 0, (3,))
+        multiply2(3, 1, (3,))
+        multiply2(3, 2, (3,))
+        times(3, 2)
+        turn(3, 2, nc.vector.tensor_copy)
+        times(3, 3)
         quantise_da(2, 0, C)
-        multiply1(1)
         multiply1(2)
-        da_part(3, 2)
+        turn(3, 3, nc.vector.tensor_copy)
         quantise_da(3, 0, C // 2)
-        da_part(3, 3)
         quantise_da(3, C // 2, C)
         multiply1(3)
 

from contextlib import ExitStack

import concourse.mybir as mybir
from concourse.masks import make_identity

K, T, E, C, H, N = 128, 1024, 4, 512, 512, 1536
P = 128
PACK = 4
SLOTS = E * C
PASSES = N // 512
QT = C // P

FLOPS = 2 * SLOTS * (N * H + H * K)
BYTES = (
    4 * N * T + 4 * H * SLOTS + E * PASSES * (128 * 1024 + 16 * 512)
    + E * (128 * 256 + 16 * 128) + 4 * SLOTS + 2 * 128 * (128 + 64 + 64) + 4 * K * T
)

F32 = mybir.dt.float32
BF16 = mybir.dt.bfloat16
I32 = mybir.dt.int32
U32 = mybir.dt.uint32
U16 = mybir.dt.uint16
U8 = mybir.dt.uint8
E5M2 = mybir.dt.float8_e5m2_x4
E2M1 = mybir.dt.float4_e2m1fn_x4
MULT = mybir.AluOpType.mult
ADD = mybir.AluOpType.add
COPY = mybir.ActivationFunctionType.Copy
RELU = mybir.ActivationFunctionType.Relu


def tile_moe_bdx_mlp_relu2_kernel(
    tc, dyT, a, w2_words, w2_scales, w1_words, w1_scales, gate, offs, pos1, pos2, out
):
    nc = tc.nc
    PAIR = 2 * C
    with ExitStack() as ctx:
        keep = ctx.enter_context(tc.tile_pool(name="keep", bufs=1))
        gathered = ctx.enter_context(tc.tile_pool(name="gathered", bufs=2))
        grouped = ctx.enter_context(tc.tile_pool(name="grouped", bufs=2))
        coded = ctx.enter_context(tc.tile_pool(name="coded", bufs=4))
        hidden = ctx.enter_context(tc.tile_pool(name="hidden", bufs=4))
        a_pool = ctx.enter_context(tc.tile_pool(name="a_pool", bufs=2))
        last_da = ctx.enter_context(tc.tile_pool(name="last_da", bufs=2))
        da_codes_pool = ctx.enter_context(tc.tile_pool(name="da_codes_pool", bufs=3))
        slope_pool = ctx.enter_context(tc.tile_pool(name="slope_pool", bufs=4))
        dh_psum = ctx.enter_context(tc.psum_pool(name="dh_psum", bufs=5))
        tr_psum = ctx.enter_context(tc.psum_pool(name="tr_psum", bufs=3))

        offs_sb = keep.tile([P, SLOTS // 16], U16, name="offs_sb")
        pos1_sb = keep.tile([P, T // 16], U16, name="pos1_sb")
        pos2_sb = keep.tile([P, T // 16], U16, name="pos2_sb")
        gates = [keep.tile([P, PAIR], F32, name=f"gate{e}") for e in range(2)]
        planes = [
            [keep.tile([P, T + 8], F32, name=f"dy{s}_{t}") for t in range(PACK)] for s in range(PASSES)
        ]
        w2_sb = [keep.tile([P, PASSES * 1024], U8, name=f"w2_{e}", align_bytes=64) for e in range(E)]
        w2_sc = keep.tile([P, E * PASSES * H], U8, name="w2_sc", align_bytes=64)
        w1_sb = keep.tile([P, E * 256], U8, name="w1_sb", align_bytes=64)
        w1_sc = keep.tile([P, E * K], U8, name="w1_sc", align_bytes=64)
        a_sb = {}
        ident = keep.tile([P, P], F32, name="ident")
        ident_bf = keep.tile([P, P], BF16, name="ident_bf")
        dx_sb = keep.tile([P, SLOTS], F32, name="dx_sb")

        for s in range(PASSES):
            for t in range(PACK):
                nc.vector.memset(planes[s][t][:, T : T + 8], 0.0)
        nc.gpsimd.memset(w2_sc[:].bitcast(I32), 0)
        nc.gpsimd.memset(w1_sc[:].bitcast(I32), 0)
        make_identity(nc, ident[:])
        make_identity(nc, ident_bf[:])

        dy_rows = dyT.rearrange("(s p t) j -> s t p j", p=P, t=PACK)

        def load_plane(s, t):
            nc.sync.dma_start(out=planes[s][t][:, 0:T], in_=dy_rows[s, t])

        def load_gate(e):
            nc.sync.dma_start(
                out=gates[e // 2][:, (e % 2) * C : (e % 2 + 1) * C], in_=gate[0:P, e * C : (e + 1) * C]
            )

        def load_w2(e):
            nc.sync.dma_start(
                out=w2_sb[e][:].bitcast(I32).rearrange("p (s w) -> p s w", s=PASSES),
                in_=w2_words.bitcast(I32)[e].rearrange("s p w -> p s w"),
            )

        def load_a(e):
            a_sb[e] = a_pool.tile([P, PACK, C], F32, name="a")
            nc.sync.dma_start(
                out=a_sb[e][:], in_=a[:, e * C : (e + 1) * C].rearrange("(p t) c -> p t c", t=PACK)
            )

        def load_scales():
            src2 = w2_scales.bitcast(I32).rearrange("e s f w -> f (e s) w")
            src1 = w1_scales.bitcast(I32).rearrange("e s f w -> f (e s) w")
            for q in range(4):
                rows = slice(32 * q, 32 * q + 4)
                nc.sync.dma_start(
                    out=w2_sc[rows, :].bitcast(I32).rearrange("f (g w) -> f g w", g=E * PASSES),
                    in_=src2[4 * q : 4 * q + 4],
                )
            for q in range(4):
                rows = slice(32 * q, 32 * q + 4)
                nc.sync.dma_start(
                    out=w1_sc[rows, :].bitcast(I32).rearrange("f (g w) -> f g w", g=E),
                    in_=src1[4 * q : 4 * q + 4],
                )

        nc.sync.dma_start(offs_sb[:], offs)
        load_gate(0)
        load_plane(0, 0)
        load_gate(1)
        for t in range(1, PACK):
            load_plane(0, t)
        load_a(0)
        for t in range(PACK):
            load_plane(1, t)
        load_a(1)
        load_gate(2)
        load_gate(3)
        for t in range(PACK):
            load_plane(2, t)

        codes = {}
        dh_banks = {}
        slopes = {}
        da_parts = {}

        def gather(g32, s, t, slot0, n):
            base = slot0 % PAIR
            here = slot0 % g32.shape[2]
            nc.vector.tensor_tensor(
                g32[:, t, here : here + n],
                planes[s][t][:].indirect(offs_sb[:, slot0 // 16 : (slot0 + n) // 16]),
                gates[slot0 // PAIR][:, base : base + n],
                MULT,
            )

        def interleave(g32, n):
            gb = grouped.tile([P, n, PACK], BF16, name="gb", align_bytes=64)
            nc.scalar.activation(
                gb[:].rearrange("p (c i) t -> p c t i", i=4),
                g32[:].rearrange("p t (c i) -> p c t i", i=4),
                COPY,
            )
            return gb

        def quantise(gb, n):
            words = coded.tile([P, n], U32, name="g_words", align_bytes=64)
            scales = coded.tile([P, n], U8, name="g_scales", align_bytes=64)
            nc.vector.quantize_mx(
                out=words[:].bitcast(E5M2),
                scales=scales[:],
                in_=gb[:].rearrange("p c t -> p (c t)"),
            )
            return words, scales

        def multiply2(e, s, qs=range(QT)):
            words, scales, base = codes[e, s]
            for q in qs:
                if s == 0:
                    dh_banks[e, q] = dh_psum.tile([P, H], F32, name="dh")
                cols = slice(base + q * P, base + (q + 1) * P)
                nc.tensor.matmul_mx(
                    out=dh_banks[e, q][:],
                    lhsT=words[:, cols].bitcast(E5M2),
                    lhsT_scale=scales[:, cols],
                    rhs=w2_sb[e][:, s * 1024 : (s + 1) * 1024].bitcast(E2M1),
                    rhs_scale=w2_sc[:, (e * PASSES + s) * H : (e * PASSES + s + 1) * H],
                    start=(s == 0),
                    stop=(s == PASSES - 1),
                )

        def slope(e):
            slopes[e] = slope_pool.tile([P, QT, PACK, P], F32, name="slope")
            for q in range(QT):
                bank = tr_psum.tile([P, PACK, P], F32, name="turned")
                for t in range(PACK):
                    nc.tensor.transpose(bank[:, t, :], a_sb[e][:, t, q * P : (q + 1) * P], ident[:])
                nc.scalar.activation(slopes[e][:, q, :, :], bank[:], RELU, scale=2.0)

        by_slot = {}

        def make_da(e):
            da_parts[e] = (
                last_da.tile([P, C, PACK], BF16, name="da", align_bytes=64),
                da_codes_pool.tile([P, C], U32, name="da_words", align_bytes=64),
                da_codes_pool.tile([P, C], U8, name="da_scales", align_bytes=64),
                0,
            )

        def times(e, q):
            if e == 2 and q >= 2:
                by_slot[e, q] = grouped.tile([P, PACK, P], BF16, name="gb", align_bytes=64)
            else:
                by_slot[e, q] = hidden.tile([P, PACK, P], BF16, name="by_slot")
            nc.vector.tensor_tensor(
                by_slot[e, q][:],
                dh_banks[e, q][:].rearrange("p (m t) -> p t m", t=PACK),
                slopes[e][:, q, :, :],
                MULT,
            )

        def turn(e, q, copy):
            if e not in da_parts:
                make_da(e)
            bank = tr_psum.tile([P, PACK, P], BF16, name="turned")
            for t in range(PACK):
                nc.tensor.transpose(bank[:, t, :], by_slot[e, q][:, t, :], ident_bf[:])
            copy(da_parts[e][0][:, q * P : (q + 1) * P, :], bank[:].rearrange("p t c -> p c t"))

        def quantise_da(e, c0, c1):
            da, words, scales, base = da_parts[e]
            nc.vector.quantize_mx(
                out=words[:, c0:c1].bitcast(E5M2),
                scales=scales[:, c0:c1],
                in_=da[:, c0:c1, :].rearrange("p c t -> p (c t)"),
            )

        def multiply1(e):
            da, words, scales, base = da_parts[e]
            dx = tr_psum.tile([P, C], F32, name="turned")
            nc.tensor.matmul_mx(
                out=dx[:],
                lhsT=w1_sb[:, e * 256 : (e + 1) * 256].bitcast(E2M1),
                lhsT_scale=w1_sc[:, e * K : (e + 1) * K],
                rhs=words[:, base : base + C].bitcast(E5M2),
                rhs_scale=scales[:, base : base + C],
                start=True,
                stop=True,
            )
            nc.scalar.activation(dx_sb[:, e * C : (e + 1) * C], dx[:], COPY)

        def finish(e):
            quantise_da(e, 0, C)
            multiply1(e)

        def pair_gathers(pair, s, g32, ts):
            for t in ts:
                if pair == 0 and s == 0 and t == 0:
                    gather(g32, s, t, 0, C)
                    gather(g32, s, t, C, C)
                else:
                    gather(g32, s, t, pair * PAIR, PAIR)

        def pair_tile():
            return gathered.tile([P, PACK, PAIR], F32, name="g32")

        def pair_codes(gb, pair, s):
            words, scales = quantise(gb, PAIR)
            for x in range(2):
                codes[2 * pair + x, s] = (words, scales, x * C)

        def interleave_half(g32):
            gb = grouped.tile([P, C, PACK], BF16, name="gb", align_bytes=64)
            nc.scalar.activation(
                gb[:].rearrange("p (c i) t -> p c t i", i=4),
                g32[:].rearrange("p t (c i) -> p c t i", i=4),
                COPY,
            )
            return gb

        g = pair_tile()
        pair_gathers(0, 0, g, range(4))
        b = interleave(g, PAIR)
        slope(0)
        load_a(2)
        load_scales()
        load_w2(0)
        load_w2(1)
        nc.sync.dma_start(
            out=w1_sb[:].bitcast(I32).rearrange("p (e w) -> p e w", e=E),
            in_=w1_words.bitcast(I32).rearrange("e s p w -> p (e s) w"),
        )
        load_w2(2)
        load_w2(3)
        nc.sync.dma_start(pos1_sb[:], pos1)
        nc.sync.dma_start(pos2_sb[:], pos2)
        for s in (1, 2):
            g = pair_tile()
            pair_gathers(0, s, g, range(3))
            pair_codes(b, 0, s - 1)
            multiply2(0, s - 1)
            pair_gathers(0, s, g, range(3, 4))
            b = interleave(g, PAIR)
            slope(s)
            if s == 1:
                load_a(3)
        def single(e, s):
            g1 = gathered.tile([P, PACK, C], F32, name="g32")
            for t in range(4):
                gather(g1, s, t, e * C, C)
            return g1

        def single_codes(e, s, gb):
            codes[e, s] = quantise(gb, C) + (0,)

        g = pair_tile()
        pair_gathers(1, 0, g, range(4))
        b_next = interleave(g, PAIR)
        pair_codes(b, 0, 2)
        b = b_next
        multiply2(0, 2)
        for q in range(QT):
            times(0, q)
        for q in range(QT):
            for s in range(PASSES):
                multiply2(1, s, (q,))
            turn(0, q, nc.scalar.copy)
        slope(3)
        g = single(2, 1)
        b21 = interleave_half(g)
        for q in range(QT):
            times(1, q)
        pair_codes(b, 1, 0)
        multiply2(2, 0)
        for q in range(QT):
            turn(1, q, nc.scalar.copy)
        quantise_da(0, 0, C)
        multiply1(0)
        g = single(2, 2)
        b22 = interleave_half(g)
        single_codes(2, 1, b21)
        multiply2(2, 1)
        quantise_da(1, 0, C)
        multiply1(1)
        g = single(3, 1)
        single_codes(2, 2, b22)
        multiply2(2, 2)
        b31 = interleave_half(g)
        for q in range(2):
            times(2, q)
            turn(2, q, nc.scalar.copy)
        multiply2(3, 0, range(2))
        HALF = C // 2
        b32 = [
            grouped.tile([P, HALF, PACK], BF16, name="gb", align_bytes=64),
            hidden.tile([P, HALF, PACK], BF16, name="b32_late", align_bytes=64),
        ]
        words32 = coded.tile([P, C], U32, name="g_words", align_bytes=64)
        scales32 = coded.tile([P, C], U8, name="g_scales", align_bytes=64)
        codes[3, 2] = (words32, scales32, 0)

        def last_gather(h):
            if h == 0:
                g1 = gathered.tile([P, PACK, HALF], F32, name="g32")
            else:
                g1 = grouped.tile([P, PACK, HALF], F32, name="gb", align_bytes=64)
            for t in range(4):
                gather(g1, 2, t, 3 * C + h * HALF, HALF)
            return g1

        def last_interleave(g1, h):
            nc.scalar.activation(
                b32[h][:].rearrange("p (c i) t -> p c t i", i=4),
                g1[:].rearrange("p t (c i) -> p c t i", i=4),
                COPY,
            )

        def last_quantise(h):
            cols = slice(h * HALF, (h + 1) * HALF)
            nc.vector.quantize_mx(
                out=words32[:, cols].bitcast(E5M2),
                scales=scales32[:, cols],
                in_=b32[h][:].rearrange("p c t -> p (c t)"),
            )

        g = last_gather(0)
        last_interleave(g, 0)
        single_codes(3, 1, b31)
        multiply2(3, 1, range(2))
        g = last_gather(1)
        last_quantise(0)
        multiply2(3, 2, range(2))
        last_interleave(g, 1)
        times(2, 2)
        turn(2, 2, nc.scalar.copy)
        for q in range(2):
            times(3, q)
            turn(3, q, nc.scalar.copy)
        multiply2(3, 0, (2,))
        multiply2(3, 1, (2,))
        last_quantise(1)
        multiply2(3, 2, (2,))
        times(2, 3)
        turn(2, 3, nc.scalar.copy)
        multiply2(3, 0, (3,))
        multiply2(3, 1, (3,))
        multiply2(3, 2, (3,))
        times(3, 2)
        turn(3, 2, nc.vector.tensor_copy)
        times(3, 3)
        quantise_da(2, 0, C)
        multiply1(2)
        turn(3, 3, nc.vector.tensor_copy)
        quantise_da(3, 0, C // 2)
        quantise_da(3, C // 2, C)
        multiply1(3)

        first = slope_pool.tile([P, T], F32, name="slope")
        second = slope_pool.tile([P, T], F32, name="slope")
        total = slope_pool.tile([P, T], F32, name="slope")
        nc.vector.tensor_copy(first[:], dx_sb[:].indirect(pos1_sb[:]))
        lo = 0
        for width, adder in ((640, nc.gpsimd), (384, nc.vector)):
            cols = slice(lo, lo + width)
            nc.vector.tensor_copy(
                second[:, cols], dx_sb[:].indirect(pos2_sb[:, lo // 16 : (lo + width) // 16])
            )
            adder.tensor_tensor(total[:, cols], first[:, cols], second[:, cols], ADD)
            nc.sync.dma_start(out=out[:, cols], in_=total[:, cols])
            lo += width
